import numpy as np
import ml_dtypes

BF16 = ml_dtypes.bfloat16


def bf(x):
    return np.asarray(x, np.float32).astype(BF16)


def f32(x):
    return np.asarray(x, np.float32)


def f64(x):
    return np.asarray(x).astype(np.float64)


def striped(idx):
    return np.tile(idx.reshape(-1, 16).T, (8, 1))


S, A, K, M, N, E, Q = 512, 128, 128, 512, 192, 1, 192


def setup_inputs():
    return {"x": bf(np.random.standard_normal((A, S))), "wd": bf(np.random.standard_normal((A, M)) / np.sqrt(A)), "y": bf(np.random.standard_normal((K, N))), "w": bf(np.random.standard_normal((K, M)) / np.sqrt(K)), "b": f32(0.5 * np.random.standard_normal((M, 1))), "offs": striped(np.random.permutation(S)[:N])}


def reference(x, wd, y, w, b, offs):
    idx = offs[:16].T.reshape(-1)
    z = f64(wd).T @ f64(x)
    z[:, idx] += f64(w).T @ f64(y)
    return np.maximum(z + f64(b), 0.0)

@@ -1,0 +1,50 @@
+import concourse.mybir as mybir
+
+BF16, F32, U16 = mybir.dt.bfloat16, mybir.dt.float32, mybir.dt.uint16
+ADD, MAX = mybir.AluOpType.add, mybir.AluOpType.max
+RELU = mybir.ActivationFunctionType.Relu
+
+P = 128
+S = 512
+M = 512
+N = 192
+BLOCKS = M // P
+
+FLOPS = 2 * P * M * S + 2 * P * M * N
+
+
+def tile_rows_fillproj_relu_kernel(tc, x, wd, y, w, b, offs, out):
+    nc = tc.nc
+    with (
+        tc.tile_pool(name="held", bufs=1) as held,
+        tc.psum_pool(name="psum", bufs=1) as psum,
+    ):
+        x_tile = held.tile([P, S], BF16)
+        wd_tile = held.tile([P, M], BF16)
+        w_tile = held.tile([P, M], BF16)
+        y_tile = held.tile([P, N], BF16)
+        offsets = held.tile([P, N // 16], U16)
+        bias = held.tile([P, BLOCKS], F32)
+        nc.sync.dma_start(x_tile[:], x)
+        nc.sync.dma_start(wd_tile[:], wd)
+        nc.sync.dma_start(w_tile[:], w)
+        nc.sync.dma_start(y_tile[:], y)
+        nc.sync.dma_start(offsets[:], offs)
+        nc.sync.dma_start(bias[:], b.rearrange("(m p) o -> p (m o)", p=P))
+
+        windows = [psum.tile([P, S], F32, name=f"window{m}") for m in range(BLOCKS)]
+        for m in range(BLOCKS):
+            nc.tensor.matmul(windows[m][:], wd_tile[:, m * P : (m + 1) * P], x_tile[:], start=True, stop=False)
+
+        for m in range(BLOCKS):
+            nc.tensor.matmul(
+                windows[m][:].indirect(offsets[:]), w_tile[:, m * P : (m + 1) * P], y_tile[:], start=False, stop=True
+            )
+
+        for m in range(BLOCKS):
+            result = held.tile([P, S], F32, name=f"result{m}")
+            if m % 2 == 0:
+                nc.vector.tensor_scalar(result[:], windows[m][:], bias[:, m : m + 1], 0.0, ADD, MAX)
+            else:
+                nc.scalar.activation(result[:], windows[m][:], RELU, bias=bias[:, m : m + 1])
+            nc.sync.dma_start(out[m * P : (m + 1) * P, :], result[:])

@@ -9,6 +9,7 @@ S = 512
 M = 512
 N = 192
 BLOCKS = M // P
+WARM_UPS = 4
 
 FLOPS = 2 * P * M * S + 2 * P * M * N
 
@@ -31,6 +32,14 @@ def tile_rows_fillproj_relu_kernel(tc, x, wd, y, w, b, offs, out):
         nc.sync.dma_start(y_tile[:], y)
         nc.sync.dma_start(offsets[:], offs)
         nc.sync.dma_start(bias[:], b.rearrange("(m p) o -> p (m o)", p=P))
+
+        zeros = held.tile([P, S], BF16)
+        nc.vector.memset(zeros[:], 0.0)
+        scratch = held.tile([P, 1], F32)
+        nc.scalar.activation(scratch[:], zeros[:, 0:1], RELU)
+        warm_bank = psum.tile([P, S], F32)
+        for i in range(WARM_UPS):
+            nc.tensor.matmul(warm_bank[:], zeros[:, 0:P], zeros[:], start=True, stop=True)
 
         windows = [psum.tile([P, S], F32, name=f"window{m}") for m in range(BLOCKS)]
         for m in range(BLOCKS):

@@ -9,7 +9,7 @@ S = 512
 M = 512
 N = 192
 BLOCKS = M // P
-WARM_UPS = 4
+WARM_UPS = 3
 
 FLOPS = 2 * P * M * S + 2 * P * M * N
 
@@ -27,9 +27,9 @@ def tile_rows_fillproj_relu_kernel(tc, x, wd, y, w, b, offs, out):
         offsets = held.tile([P, N // 16], U16)
         bias = held.tile([P, BLOCKS], F32)
         nc.sync.dma_start(x_tile[:], x)
-        nc.sync.dma_start(wd_tile[:], wd)
-        nc.sync.dma_start(w_tile[:], w)
+        nc.scalar.dma_start(wd_tile[:], wd)
         nc.sync.dma_start(y_tile[:], y)
+        nc.scalar.dma_start(w_tile[:], w)
         nc.sync.dma_start(offsets[:], offs)
         nc.sync.dma_start(bias[:], b.rearrange("(m p) o -> p (m o)", p=P))
 
@@ -51,9 +51,11 @@ def tile_rows_fillproj_relu_kernel(tc, x, wd, y, w, b, offs, out):
             )
 
         for m in range(BLOCKS):
-            result = held.tile([P, S], F32, name=f"result{m}")
-            if m % 2 == 0:
-                nc.vector.tensor_scalar(result[:], windows[m][:], bias[:, m : m + 1], 0.0, ADD, MAX)
-            else:
-                nc.scalar.activation(result[:], windows[m][:], RELU, bias=bias[:, m : m + 1])
-            nc.sync.dma_start(out[m * P : (m + 1) * P, :], result[:])
+            for h in range(2):
+                cols = slice(h * S // 2, (h + 1) * S // 2)
+                result = held.tile([P, S // 2], F32, name=f"result{m}_{h}")
+                if m % 2 == 0:
+                    nc.vector.tensor_scalar(result[:], windows[m][:, cols], bias[:, m : m + 1], 0.0, ADD, MAX)
+                else:
+                    nc.scalar.activation(result[:], windows[m][:, cols], RELU, bias=bias[:, m : m + 1])
+                nc.sync.dma_start(out[m * P : (m + 1) * P, cols], result[:])

import concourse.mybir as mybir

BF16, F32, U16 = mybir.dt.bfloat16, mybir.dt.float32, mybir.dt.uint16
ADD, MAX = mybir.AluOpType.add, mybir.AluOpType.max
RELU = mybir.ActivationFunctionType.Relu

P = 128
S = 512
M = 512
N = 192
BLOCKS = M // P
WARM_UPS = 3

FLOPS = 2 * P * M * S + 2 * P * M * N


def tile_rows_fillproj_relu_kernel(tc, x, wd, y, w, b, offs, out):
    nc = tc.nc
    with (
        tc.tile_pool(name="held", bufs=1) as held,
        tc.psum_pool(name="psum", bufs=1) as psum,
    ):
        x_tile = held.tile([P, S], BF16)
        wd_tile = held.tile([P, M], BF16)
        w_tile = held.tile([P, M], BF16)
        y_tile = held.tile([P, N], BF16)
        offsets = held.tile([P, N // 16], U16)
        bias = held.tile([P, BLOCKS], F32)
        nc.sync.dma_start(x_tile[:], x)
        nc.scalar.dma_start(wd_tile[:], wd)
        nc.sync.dma_start(y_tile[:], y)
        nc.scalar.dma_start(w_tile[:], w)
        nc.sync.dma_start(offsets[:], offs)
        nc.sync.dma_start(bias[:], b.rearrange("(m p) o -> p (m o)", p=P))

        zeros = held.tile([P, S], BF16)
        nc.vector.memset(zeros[:], 0.0)
        scratch = held.tile([P, 1], F32)
        nc.scalar.activation(scratch[:], zeros[:, 0:1], RELU)
        warm_bank = psum.tile([P, S], F32)
        for i in range(WARM_UPS):
            nc.tensor.matmul(warm_bank[:], zeros[:, 0:P], zeros[:], start=True, stop=True)

        windows = [psum.tile([P, S], F32, name=f"window{m}") for m in range(BLOCKS)]
        for m in range(BLOCKS):
            nc.tensor.matmul(windows[m][:], wd_tile[:, m * P : (m + 1) * P], x_tile[:], start=True, stop=False)

        for m in range(BLOCKS):
            nc.tensor.matmul(
                windows[m][:].indirect(offsets[:]), w_tile[:, m * P : (m + 1) * P], y_tile[:], start=False, stop=True
            )

        for m in range(BLOCKS):
            for h in range(2):
                cols = slice(h * S // 2, (h + 1) * S // 2)
                result = held.tile([P, S // 2], F32, name=f"result{m}_{h}")
                if m % 2 == 0:
                    nc.vector.tensor_scalar(result[:], windows[m][:, cols], bias[:, m : m + 1], 0.0, ADD, MAX)
                else:
                    nc.scalar.activation(result[:], windows[m][:, cols], RELU, bias=bias[:, m : m + 1])
                nc.sync.dma_start(out[m * P : (m + 1) * P, cols], result[:])
